import numpy as np
import ml_dtypes


def mxq(x, axis, fmt="e4m3"):
    dtype, down = {"e4m3": (ml_dtypes.float8_e4m3fn, 7), "e5m2": (ml_dtypes.float8_e5m2, 14)}[fmt]
    v = np.moveaxis(np.asarray(x, np.float32).astype(ml_dtypes.bfloat16).astype(np.float64), axis, -1)
    blocks = v.reshape(v.shape[:-1] + (-1, 32))
    amax = np.abs(blocks).max(-1, keepdims=True)
    byte = np.maximum(np.where(amax > 0, np.frexp(amax)[1] - 1 + 127, 0) - down, 1)
    scale = np.exp2(byte - 127.0)
    codes = (blocks / scale).astype(np.float32).astype(dtype).astype(np.float64)
    return np.moveaxis((codes * scale).reshape(v.shape), -1, axis)


WIDE = False


def mx_kscale(k):
    if not WIDE:
        return np.ones(k)
    levels = np.array([30, -30])
    if k % 512:
        return np.exp2(np.random.permutation(np.resize(levels, k // 32))).repeat(32)
    a = np.empty((k // 512, 16))
    for p in range(k // 512):
        a[p, :8] = np.random.permutation(np.resize(levels, 8))
        for g in range(8):
            far = levels[np.abs(levels - a[p, g]) >= 10]
            a[p, g + 8] = far[np.random.randint(len(far))]
    return np.exp2(a.ravel()).repeat(32)


def f64(x):
    return np.asarray(x).astype(np.float64)


def striped(idx):
    return np.tile(np.asarray(idx).reshape(-1, 16).T, (8, 1)).astype(np.uint16)


def unstriped(offs):
    return offs[:16].T.reshape(-1).astype(np.int64)


E2M1 = np.array([0.0, 0.5, 1.0, 1.5, 2.0, 3.0, 4.0, 6.0, -0.0, -0.5, -1.0, -1.5, -2.0, -3.0, -4.0, -6.0])


def pack_weight(w, fmt):
    k, n = w.shape
    w = f64(np.asarray(w, np.float32).astype(ml_dtypes.bfloat16)).reshape(k // 32, 32, n)
    amax = np.abs(w).max(1)
    if fmt in ("e4m3", "e5m2"):
        byte = np.frexp(amax)[1] - 1 + 127 - (7 if fmt == "e4m3" else 14)
    else:
        mant, ex = np.frexp(amax / 6.0)
        byte = np.where(mant > 0.5, ex, ex - 1) + 127
    byte = np.clip(np.where(amax > 0, byte, 1), 1, 254)
    scaled = (w * np.exp2(127.0 - byte)[:, None, :]).reshape(k, n).astype(np.float32)
    by_word = np.ascontiguousarray(scaled.reshape(k // 512, 128, 4, n).transpose(0, 1, 3, 2))
    if fmt in ("e4m3", "e5m2"):
        words = by_word.astype(ml_dtypes.float8_e4m3fn if fmt == "e4m3" else ml_dtypes.float8_e5m2).view(np.uint8)
    else:
        c = by_word.astype(ml_dtypes.float4_e2m1fn).view(np.uint8) & 0xF
        words = (c[..., 0::2] | (c[..., 1::2] << 4)).reshape(k // 512, 128, 2 * n)
    return np.ascontiguousarray(words), np.ascontiguousarray(byte.astype(np.uint8).reshape(k // 512, 16, n))


def unpack_weight(words, scales, fmt):
    g, _, n = scales.shape
    words = np.ascontiguousarray(words).reshape(g, 128, n, -1)
    if fmt in ("e4m3", "e5m2"):
        vals = words.view(ml_dtypes.float8_e4m3fn if fmt == "e4m3" else ml_dtypes.float8_e5m2).astype(np.float64)
    else:
        nib = np.empty((g, 128, n, 4), np.uint8)
        nib[..., 0::2] = words & 0xF
        nib[..., 1::2] = words >> 4
        vals = E2M1[nib]
    vals = vals * np.repeat(np.exp2(scales.astype(np.float64) - 127.0), 8, axis=1)[..., None]
    return vals.transpose(0, 1, 3, 2).reshape(g * 512, n)


def sigmoid(v):
    return 1.0 / (1.0 + np.exp(-v))


K, T, J, R, O, N = 512, 1024, 256, 512, 128, 256


def setup_inputs():
    n = np.random.standard_normal
    idx = np.random.permutation(T)[:J]
    idx2 = np.random.permutation(J)[:O]
    idx3 = np.random.permutation(J)[:O]
    fk = mx_kscale(K)
    fr = mx_kscale(R)
    xtp = pack_weight(n((K, T)) / fk[:, None], "e4m3")
    wp = pack_weight(n((K, R)) * 1 / np.sqrt(K) * fk[:, None], "e2m1")
    w2p = pack_weight(n((K, R)) * 1 / np.sqrt(K) * fk[:, None] * fr, "e5m2")
    wbp = pack_weight(n((R, N)) * 1 / np.sqrt(R) / fr[:, None], "e5m2")
    return {
        "xt_words": xtp[0],
        "xt_scales": xtp[1],
        "w_words": wp[0],
        "w_scales": wp[1],
        "w2_words": w2p[0],
        "w2_scales": w2p[1],
        "sg": (np.random.uniform(0.6, 1.6, (R, 1))).astype(np.float32),
        "bg": (np.random.uniform(-1.0, 1.0, (R, 1))).astype(np.float32),
        "wb_words": wbp[0],
        "wb_scales": wbp[1],
        "offs": striped(idx),
        "offs2": striped(idx2),
        "offs3": striped(idx3),
    }


def reference(xt_words, xt_scales, w_words, w_scales, w2_words, w2_scales, sg, bg, wb_words, wb_scales, offs, offs2, offs3):
    idx = unstriped(offs)
    idx2 = unstriped(offs2)
    idx3 = unstriped(offs3)
    xtu = unpack_weight(xt_words, xt_scales, "e4m3")
    wu = unpack_weight(w_words, w_scales, "e2m1")
    w2u = unpack_weight(w2_words, w2_scales, "e5m2")
    wbu = unpack_weight(wb_words, wb_scales, "e5m2")
    xtidxg = xtu[:, idx]
    a = wu.T @ xtidxg
    b = w2u.T @ xtidxg
    hid = b[:, idx3] * sigmoid(a[:, idx2] * f64(sg) + f64(bg))
    hidq = mxq(hid, 0, "e4m3")
    y = wbu.T @ hidq
    return y

@@ -1,0 +1,174 @@
+from contextlib import ExitStack
+
+import concourse.mybir as mybir
+
+K, T, J, R, O, N = 512, 1024, 256, 512, 128, 256
+FLOPS = 2 * (2 * K * R * J + R * N * O)
+
+F32 = mybir.dt.float32
+BF16 = mybir.dt.bfloat16
+I32 = mybir.dt.int32
+U32 = mybir.dt.uint32
+U16 = mybir.dt.uint16
+U8 = mybir.dt.uint8
+E4M3 = mybir.dt.float8_e4m3fn_x4
+E5M2 = mybir.dt.float8_e5m2_x4
+E2M1 = mybir.dt.float4_e2m1fn_x4
+ACT = mybir.ActivationFunctionType
+MULT = mybir.AluOpType.mult
+
+P = 128
+PACK = 4
+
+
+def load_scale_row(queue, plane, scales, i):
+    queue.dma_start(out=plane[i:P:32, :].bitcast(I32), in_=scales[0, i:16:4, :].bitcast(I32))
+
+
+def tile_list_twow_gatefetch_one_plain_kernel(
+    tc, xt_words, xt_scales, w_words, w_scales, w2_words, w2_scales, sg, bg, wb_words, wb_scales, offs, offs2, offs3, out
+):
+    nc = tc.nc
+    with ExitStack() as ctx:
+        keep = ctx.enter_context(tc.tile_pool(name="keep", bufs=1))
+        psum = ctx.enter_context(tc.psum_pool(name="psum", bufs=8))
+
+        tokens = keep.tile([P, J // 16], U16, name="tokens")
+        gate_slots = keep.tile([P, O // 16], U16, name="gate_slots")
+        value_slots = keep.tile([P, O // 16], U16, name="value_slots")
+        x_words = keep.tile([P, T], U32, name="x_words", align_bytes=64)
+        x_plane = keep.tile([P, T], U8, name="x_plane", align_bytes=64)
+        w_raw = keep.tile([P, R], U16, name="w_raw", align_bytes=64)
+        staged = keep.tile([16, 2 * R // 4], I32, name="staged")
+        planes_raw = keep.tile([P, 2 * R], U8, name="planes_raw", align_bytes=64)
+        w2_raw = keep.tile([P, R], U32, name="w2_raw", align_bytes=64)
+        wb_codes = keep.tile([P, N], U32, name="wb_codes", align_bytes=64)
+        wb_plane = keep.tile([P, N], U8, name="wb_plane", align_bytes=64)
+        slope = keep.tile([P, PACK], F32, name="slope")
+        offset = keep.tile([P, PACK], F32, name="offset")
+
+        nc.vector.memset(x_plane[:, 0 : T // 2].bitcast(I32), 0)
+        nc.gpsimd.memset(x_plane[:, T // 2 : T].bitcast(I32), 0)
+        nc.vector.memset(planes_raw[:].bitcast(I32), 0)
+        nc.vector.memset(wb_plane[:].bitcast(I32), 0)
+
+        nc.sync.dma_start(tokens[:], offs)
+        nc.gpsimd.dma_start(out=w_raw[:].bitcast(I32), in_=w_words[0].bitcast(I32))
+        nc.sync.dma_start(out=staged[:, 0 : R // 4], in_=w_scales[0].bitcast(I32))
+        nc.sync.dma_start(out=staged[:, R // 4 : R // 2], in_=w2_scales[0].bitcast(I32))
+        load_scale_row(nc.sync, x_plane, xt_scales, 0)
+        load_scale_row(nc.sync, x_plane, xt_scales, 1)
+        load_scale_row(nc.scalar, x_plane, xt_scales, 2)
+        load_scale_row(nc.scalar, x_plane, xt_scales, 3)
+        nc.sync.dma_start(out=x_words[:].bitcast(I32), in_=xt_words[0].rearrange("p t b -> p (t b)").bitcast(I32))
+        nc.gpsimd.dma_start(out=offset[:], in_=bg.rearrange("(p t) o -> p (t o)", t=PACK))
+        nc.sync.dma_start(out=planes_raw[0:P:32, :].bitcast(I32), in_=staged[0:16:4, :])
+        nc.sync.dma_start(out=planes_raw[1:P:32, :].bitcast(I32), in_=staged[1:16:4, :])
+        nc.sync.dma_start(out=planes_raw[2:P:32, :].bitcast(I32), in_=staged[2:16:4, :])
+        nc.sync.dma_start(out=planes_raw[3:P:32, :].bitcast(I32), in_=staged[3:16:4, :])
+        nc.sync.dma_start(out=w2_raw[:].bitcast(I32), in_=w2_words[0].rearrange("p r b -> p (r b)").bitcast(I32))
+        nc.sync.dma_start(gate_slots[:], offs2)
+        nc.sync.dma_start(out=slope[:], in_=sg.rearrange("(p t) o -> p (t o)", t=PACK))
+        nc.sync.dma_start(value_slots[:], offs3)
+        nc.sync.dma_start(out=wb_codes[:].bitcast(I32), in_=wb_words[0].rearrange("p n b -> p (n b)").bitcast(I32))
+        load_scale_row(nc.sync, wb_plane, wb_scales, 0)
+        load_scale_row(nc.sync, wb_plane, wb_scales, 1)
+        load_scale_row(nc.sync, wb_plane, wb_scales, 2)
+        load_scale_row(nc.sync, wb_plane, wb_scales, 3)
+
+        xg_plane = keep.tile([P, J], U8, name="xg_plane", align_bytes=64)
+        xg_words = keep.tile([P, J], U32, name="xg_words", align_bytes=64)
+        w_codes = keep.tile([P, R], U16, name="w_codes", align_bytes=64)
+        w_plane = keep.tile([P, R], U8, name="w_plane", align_bytes=64)
+        w2_codes = keep.tile([P, R], U32, name="w2_codes", align_bytes=64)
+        w2_plane = keep.tile([P, R], U8, name="w2_plane", align_bytes=64)
+
+        def deal(copy, dst, src, first=0, last=PACK):
+            copy(
+                out=dst[:].rearrange("p (t m) -> p t m", t=PACK)[:, first:last, :],
+                in_=src.rearrange("p (m t) -> p t m", t=PACK)[:, first:last, :],
+            )
+
+        deal(nc.scalar.copy, w_codes, w_raw[:])
+        nc.vector.tensor_copy(out=xg_plane[:], in_=x_plane[:].indirect(tokens[:]))
+        nc.vector.tensor_copy(out=xg_words[:], in_=x_words[:].indirect(tokens[:]))
+        deal(nc.vector.tensor_copy, w_plane, planes_raw[:, 0:R], 0, 2)
+        deal(nc.vector.tensor_copy, w_plane, planes_raw[:, 0:R], 2, 4)
+        deal(nc.scalar.copy, w2_codes, w2_raw[:])
+        deal(nc.vector.tensor_copy, w2_plane, planes_raw[:, R : 2 * R])
+
+        gate = keep.tile([P, PACK, O], F32, name="gate")
+        value = keep.tile([P, PACK, O], F32, name="value")
+
+        def product(codes, fmt, plane, t):
+            cols = slice(t * P, (t + 1) * P)
+            acc = psum.tile([P, J], F32, name="acc")
+            nc.tensor.matmul_mx(
+                out=acc[:],
+                lhsT=codes[:, cols].bitcast(fmt),
+                lhsT_scale=plane[:, cols],
+                rhs=xg_words[:].bitcast(E4M3),
+                rhs_scale=xg_plane[:],
+                start=True,
+                stop=True,
+            )
+            return acc
+
+        a_accs = [product(w_codes, E2M1, w_plane, t) for t in range(PACK)]
+        for t in range(PACK):
+            a_rows = keep.tile([P, J], F32, name="a_rows%d" % t)
+            copy = nc.scalar.copy if t % 2 == 0 else nc.vector.tensor_copy
+            copy(out=a_rows[:], in_=a_accs[t][:])
+            nc.scalar.activation(
+                out=gate[:, t, :],
+                in_=a_rows[:].indirect(gate_slots[:]),
+                func=ACT.Sigmoid,
+                bias=offset[:, t : t + 1],
+                scale=slope[:, t : t + 1],
+            )
+        b_accs = [product(w2_codes, E5M2, w2_plane, t) for t in range(PACK)]
+        for t in range(PACK):
+            b_rows = keep.tile([P, J], F32, name="b_rows%d" % t)
+            nc.vector.tensor_copy(out=b_rows[:], in_=b_accs[t][:])
+            if t < 2:
+                nc.scalar.activation(out=value[:, t, :], in_=b_rows[:].indirect(value_slots[:]), func=ACT.Copy)
+            else:
+                nc.vector.tensor_copy(out=value[:, t, :], in_=b_rows[:].indirect(value_slots[:]))
+
+        hid = keep.tile([P, O, PACK], BF16, name="hid", align_bytes=64)
+        hid_codes = keep.tile([P, O], U32, name="hid_codes", align_bytes=64)
+        hid_plane = keep.tile([P, O], U8, name="hid_plane", align_bytes=64)
+        halves = [slice(0, O // 2), slice(O // 2, O)]
+        for half in halves:
+            nc.vector.tensor_tensor(
+                out=hid[:, half, :],
+                in0=value[:, :, half].rearrange("p t o -> p o t"),
+                in1=gate[:, :, half].rearrange("p t o -> p o t"),
+                op=MULT,
+            )
+        for half in halves:
+            nc.vector.quantize_mx(
+                out=hid_codes[:, half].bitcast(E4M3),
+                scales=hid_plane[:, half],
+                in_=hid[:, half, :].rearrange("p o t -> p (o t)"),
+            )
+
+        for h in range(N // P):
+            cols = slice(h * P, (h + 1) * P)
+            acc = psum.tile([P, J], F32, name="acc")
+            nc.tensor.matmul_mx(
+                out=acc[:, 0:O],
+                lhsT=wb_codes[:, cols].bitcast(E5M2),
+                lhsT_scale=wb_plane[:, cols],
+                rhs=hid_codes[:].bitcast(E4M3),
+                rhs_scale=hid_plane[:],
+                start=True,
+                stop=True,
+            )
+            result = keep.tile([P, O], F32, name="result%d" % h)
+            if h == 0:
+                nc.scalar.copy(out=result[:], in_=acc[:, 0:O])
+                nc.scalar.dma_start(out=out[cols, :], in_=result[:])
+            else:
+                nc.vector.tensor_copy(out=result[:], in_=acc[:, 0:O])
+                nc.sync.dma_start(out=out[cols, :], in_=result[:])

@@ -76,6 +76,10 @@ def tile_list_twow_gatefetch_one_plain_kernel(
         load_scale_row(nc.sync, wb_plane, wb_scales, 2)
         load_scale_row(nc.sync, wb_plane, wb_scales, 3)
 
+        warm = keep.tile([P, 2], F32, name="warm")
+        nc.vector.memset(warm[:, 0:1], 0.0)
+        nc.scalar.activation(out=warm[:, 1:2], in_=warm[:, 0:1], func=ACT.Sigmoid)
+
         xg_plane = keep.tile([P, J], U8, name="xg_plane", align_bytes=64)
         xg_words = keep.tile([P, J], U32, name="xg_words", align_bytes=64)
         w_codes = keep.tile([P, R], U16, name="w_codes", align_bytes=64)

@@ -52,21 +52,21 @@ def tile_list_twow_gatefetch_one_plain_kernel(
         nc.vector.memset(planes_raw[:].bitcast(I32), 0)
         nc.vector.memset(wb_plane[:].bitcast(I32), 0)
 
+        nc.sync.dma_start(out=staged[:, 0 : R // 4], in_=w_scales[0].bitcast(I32))
+        nc.scalar.dma_start(out=staged[:, R // 4 : R // 2], in_=w2_scales[0].bitcast(I32))
         nc.sync.dma_start(tokens[:], offs)
         nc.gpsimd.dma_start(out=w_raw[:].bitcast(I32), in_=w_words[0].bitcast(I32))
-        nc.sync.dma_start(out=staged[:, 0 : R // 4], in_=w_scales[0].bitcast(I32))
-        nc.sync.dma_start(out=staged[:, R // 4 : R // 2], in_=w2_scales[0].bitcast(I32))
         load_scale_row(nc.sync, x_plane, xt_scales, 0)
         load_scale_row(nc.sync, x_plane, xt_scales, 1)
         load_scale_row(nc.scalar, x_plane, xt_scales, 2)
         load_scale_row(nc.scalar, x_plane, xt_scales, 3)
         nc.sync.dma_start(out=x_words[:].bitcast(I32), in_=xt_words[0].rearrange("p t b -> p (t b)").bitcast(I32))
         nc.gpsimd.dma_start(out=offset[:], in_=bg.rearrange("(p t) o -> p (t o)", t=PACK))
+        nc.sync.dma_start(out=w2_raw[:].bitcast(I32), in_=w2_words[0].rearrange("p r b -> p (r b)").bitcast(I32))
         nc.sync.dma_start(out=planes_raw[0:P:32, :].bitcast(I32), in_=staged[0:16:4, :])
         nc.sync.dma_start(out=planes_raw[1:P:32, :].bitcast(I32), in_=staged[1:16:4, :])
         nc.sync.dma_start(out=planes_raw[2:P:32, :].bitcast(I32), in_=staged[2:16:4, :])
         nc.sync.dma_start(out=planes_raw[3:P:32, :].bitcast(I32), in_=staged[3:16:4, :])
-        nc.sync.dma_start(out=w2_raw[:].bitcast(I32), in_=w2_words[0].rearrange("p r b -> p (r b)").bitcast(I32))
         nc.sync.dma_start(gate_slots[:], offs2)
         nc.sync.dma_start(out=slope[:], in_=sg.rearrange("(p t) o -> p (t o)", t=PACK))
         nc.sync.dma_start(value_slots[:], offs3)
@@ -93,12 +93,16 @@ def tile_list_twow_gatefetch_one_plain_kernel(
                 in_=src.rearrange("p (m t) -> p t m", t=PACK)[:, first:last, :],
             )
 
-        deal(nc.scalar.copy, w_codes, w_raw[:])
+        nc.scalar.copy(
+            out=w_codes[:].rearrange("p (t m) -> p m t", t=PACK), in_=w_raw[:].rearrange("p (m t) -> p m t", t=PACK)
+        )
         nc.vector.tensor_copy(out=xg_plane[:], in_=x_plane[:].indirect(tokens[:]))
         nc.vector.tensor_copy(out=xg_words[:], in_=x_words[:].indirect(tokens[:]))
         deal(nc.vector.tensor_copy, w_plane, planes_raw[:, 0:R], 0, 2)
         deal(nc.vector.tensor_copy, w_plane, planes_raw[:, 0:R], 2, 4)
-        deal(nc.scalar.copy, w2_codes, w2_raw[:])
+        nc.scalar.copy(
+            out=w2_codes[:].rearrange("p (t m) -> p m t", t=PACK), in_=w2_raw[:].rearrange("p (m t) -> p m t", t=PACK)
+        )
         deal(nc.vector.tensor_copy, w2_plane, planes_raw[:, R : 2 * R])
 
         gate = keep.tile([P, PACK, O], F32, name="gate")
@@ -145,9 +149,9 @@ def tile_list_twow_gatefetch_one_plain_kernel(
         halves = [slice(0, O // 2), slice(O // 2, O)]
         for half in halves:
             nc.vector.tensor_tensor(
-                out=hid[:, half, :],
-                in0=value[:, :, half].rearrange("p t o -> p o t"),
-                in1=gate[:, :, half].rearrange("p t o -> p o t"),
+                out=hid[:, half, :].rearrange("p (c i) t -> p c t i", i=4),
+                in0=value[:, :, half].rearrange("p t (c i) -> p c t i", i=4),
+                in1=gate[:, :, half].rearrange("p t (c i) -> p c t i", i=4),
                 op=MULT,
             )
         for half in halves:

@@ -40,7 +40,7 @@ def tile_list_twow_gatefetch_one_plain_kernel(
         x_plane = keep.tile([P, T], U8, name="x_plane", align_bytes=64)
         w_raw = keep.tile([P, R], U16, name="w_raw", align_bytes=64)
         staged = keep.tile([16, 2 * R // 4], I32, name="staged")
-        planes_raw = keep.tile([P, 2 * R], U8, name="planes_raw", align_bytes=64)
+        planes_raw = keep.tile([P, 2 * R], U8, name="planes_raw", tag="dealt", align_bytes=64)
         w2_raw = keep.tile([P, R], U32, name="w2_raw", align_bytes=64)
         wb_codes = keep.tile([P, N], U32, name="wb_codes", align_bytes=64)
         wb_plane = keep.tile([P, N], U8, name="wb_plane", align_bytes=64)
@@ -55,14 +55,14 @@ def tile_list_twow_gatefetch_one_plain_kernel(
         nc.sync.dma_start(out=staged[:, 0 : R // 4], in_=w_scales[0].bitcast(I32))
         nc.scalar.dma_start(out=staged[:, R // 4 : R // 2], in_=w2_scales[0].bitcast(I32))
         nc.sync.dma_start(tokens[:], offs)
-        nc.gpsimd.dma_start(out=w_raw[:].bitcast(I32), in_=w_words[0].bitcast(I32))
+        nc.gpsimd.dma_start(out=offset[:], in_=bg.rearrange("(p t) o -> p (t o)", t=PACK))
         load_scale_row(nc.sync, x_plane, xt_scales, 0)
         load_scale_row(nc.sync, x_plane, xt_scales, 1)
         load_scale_row(nc.scalar, x_plane, xt_scales, 2)
         load_scale_row(nc.scalar, x_plane, xt_scales, 3)
         nc.sync.dma_start(out=x_words[:].bitcast(I32), in_=xt_words[0].rearrange("p t b -> p (t b)").bitcast(I32))
-        nc.gpsimd.dma_start(out=offset[:], in_=bg.rearrange("(p t) o -> p (t o)", t=PACK))
-        nc.sync.dma_start(out=w2_raw[:].bitcast(I32), in_=w2_words[0].rearrange("p r b -> p (r b)").bitcast(I32))
+        nc.gpsimd.dma_start(out=w2_raw[:].bitcast(I32), in_=w2_words[0].rearrange("p r b -> p (r b)").bitcast(I32))
+        nc.sync.dma_start(out=w_raw[:].bitcast(I32), in_=w_words[0].bitcast(I32))
         nc.sync.dma_start(out=planes_raw[0:P:32, :].bitcast(I32), in_=staged[0:16:4, :])
         nc.sync.dma_start(out=planes_raw[1:P:32, :].bitcast(I32), in_=staged[1:16:4, :])
         nc.sync.dma_start(out=planes_raw[2:P:32, :].bitcast(I32), in_=staged[2:16:4, :])
@@ -84,7 +84,7 @@ def tile_list_twow_gatefetch_one_plain_kernel(
         xg_words = keep.tile([P, J], U32, name="xg_words", align_bytes=64)
         w_codes = keep.tile([P, R], U16, name="w_codes", align_bytes=64)
         w_plane = keep.tile([P, R], U8, name="w_plane", align_bytes=64)
-        w2_codes = keep.tile([P, R], U32, name="w2_codes", align_bytes=64)
+        w2_codes = keep.tile([P, R], U32, name="w2_codes", tag="dealt", align_bytes=64)
         w2_plane = keep.tile([P, R], U8, name="w2_plane", align_bytes=64)
 
         def deal(copy, dst, src, first=0, last=PACK):
@@ -100,10 +100,10 @@ def tile_list_twow_gatefetch_one_plain_kernel(
         nc.vector.tensor_copy(out=xg_words[:], in_=x_words[:].indirect(tokens[:]))
         deal(nc.vector.tensor_copy, w_plane, planes_raw[:, 0:R], 0, 2)
         deal(nc.vector.tensor_copy, w_plane, planes_raw[:, 0:R], 2, 4)
-        nc.scalar.copy(
+        deal(nc.vector.tensor_copy, w2_plane, planes_raw[:, R : 2 * R])
+        nc.vector.tensor_copy(
             out=w2_codes[:].rearrange("p (t m) -> p m t", t=PACK), in_=w2_raw[:].rearrange("p (m t) -> p m t", t=PACK)
         )
-        deal(nc.vector.tensor_copy, w2_plane, planes_raw[:, R : 2 * R])
 
         gate = keep.tile([P, PACK, O], F32, name="gate")
         value = keep.tile([P, PACK, O], F32, name="value")
@@ -125,7 +125,7 @@ def tile_list_twow_gatefetch_one_plain_kernel(
         a_accs = [product(w_codes, E2M1, w_plane, t) for t in range(PACK)]
         for t in range(PACK):
             a_rows = keep.tile([P, J], F32, name="a_rows%d" % t)
-            copy = nc.scalar.copy if t % 2 == 0 else nc.vector.tensor_copy
+            copy = nc.scalar.copy if t < 2 else nc.vector.tensor_copy
             copy(out=a_rows[:], in_=a_accs[t][:])
             nc.scalar.activation(
                 out=gate[:, t, :],
@@ -138,7 +138,7 @@ def tile_list_twow_gatefetch_one_plain_kernel(
         for t in range(PACK):
             b_rows = keep.tile([P, J], F32, name="b_rows%d" % t)
             nc.vector.tensor_copy(out=b_rows[:], in_=b_accs[t][:])
-            if t < 2:
+            if t < PACK - 1:
                 nc.scalar.activation(out=value[:, t, :], in_=b_rows[:].indirect(value_slots[:]), func=ACT.Copy)
             else:
                 nc.vector.tensor_copy(out=value[:, t, :], in_=b_rows[:].indirect(value_slots[:]))

@@ -61,14 +61,14 @@ def tile_list_twow_gatefetch_one_plain_kernel(
         load_scale_row(nc.scalar, x_plane, xt_scales, 2)
         load_scale_row(nc.scalar, x_plane, xt_scales, 3)
         nc.sync.dma_start(out=x_words[:].bitcast(I32), in_=xt_words[0].rearrange("p t b -> p (t b)").bitcast(I32))
-        nc.gpsimd.dma_start(out=w2_raw[:].bitcast(I32), in_=w2_words[0].rearrange("p r b -> p (r b)").bitcast(I32))
+        nc.gpsimd.dma_start(out=slope[:], in_=sg.rearrange("(p t) o -> p (t o)", t=PACK))
         nc.sync.dma_start(out=w_raw[:].bitcast(I32), in_=w_words[0].bitcast(I32))
         nc.sync.dma_start(out=planes_raw[0:P:32, :].bitcast(I32), in_=staged[0:16:4, :])
         nc.sync.dma_start(out=planes_raw[1:P:32, :].bitcast(I32), in_=staged[1:16:4, :])
         nc.sync.dma_start(out=planes_raw[2:P:32, :].bitcast(I32), in_=staged[2:16:4, :])
         nc.sync.dma_start(out=planes_raw[3:P:32, :].bitcast(I32), in_=staged[3:16:4, :])
+        nc.sync.dma_start(out=w2_raw[:].bitcast(I32), in_=w2_words[0].rearrange("p r b -> p (r b)").bitcast(I32))
         nc.sync.dma_start(gate_slots[:], offs2)
-        nc.sync.dma_start(out=slope[:], in_=sg.rearrange("(p t) o -> p (t o)", t=PACK))
         nc.sync.dma_start(value_slots[:], offs3)
         nc.sync.dma_start(out=wb_codes[:].bitcast(I32), in_=wb_words[0].rearrange("p n b -> p (n b)").bitcast(I32))
         load_scale_row(nc.sync, wb_plane, wb_scales, 0)

from contextlib import ExitStack

import concourse.mybir as mybir

K, T, J, R, O, N = 512, 1024, 256, 512, 128, 256
FLOPS = 2 * (2 * K * R * J + R * N * O)

F32 = mybir.dt.float32
BF16 = mybir.dt.bfloat16
I32 = mybir.dt.int32
U32 = mybir.dt.uint32
U16 = mybir.dt.uint16
U8 = mybir.dt.uint8
E4M3 = mybir.dt.float8_e4m3fn_x4
E5M2 = mybir.dt.float8_e5m2_x4
E2M1 = mybir.dt.float4_e2m1fn_x4
ACT = mybir.ActivationFunctionType
MULT = mybir.AluOpType.mult

P = 128
PACK = 4


def load_scale_row(queue, plane, scales, i):
    queue.dma_start(out=plane[i:P:32, :].bitcast(I32), in_=scales[0, i:16:4, :].bitcast(I32))


def tile_list_twow_gatefetch_one_plain_kernel(
    tc, xt_words, xt_scales, w_words, w_scales, w2_words, w2_scales, sg, bg, wb_words, wb_scales, offs, offs2, offs3, out
):
    nc = tc.nc
    with ExitStack() as ctx:
        keep = ctx.enter_context(tc.tile_pool(name="keep", bufs=1))
        psum = ctx.enter_context(tc.psum_pool(name="psum", bufs=8))

        tokens = keep.tile([P, J // 16], U16, name="tokens")
        gate_slots = keep.tile([P, O // 16], U16, name="gate_slots")
        value_slots = keep.tile([P, O // 16], U16, name="value_slots")
        x_words = keep.tile([P, T], U32, name="x_words", align_bytes=64)
        x_plane = keep.tile([P, T], U8, name="x_plane", align_bytes=64)
        w_raw = keep.tile([P, R], U16, name="w_raw", align_bytes=64)
        staged = keep.tile([16, 2 * R // 4], I32, name="staged")
        planes_raw = keep.tile([P, 2 * R], U8, name="planes_raw", tag="dealt", align_bytes=64)
        w2_raw = keep.tile([P, R], U32, name="w2_raw", align_bytes=64)
        wb_codes = keep.tile([P, N], U32, name="wb_codes", align_bytes=64)
        wb_plane = keep.tile([P, N], U8, name="wb_plane", align_bytes=64)
        slope = keep.tile([P, PACK], F32, name="slope")
        offset = keep.tile([P, PACK], F32, name="offset")

        nc.vector.memset(x_plane[:, 0 : T // 2].bitcast(I32), 0)
        nc.gpsimd.memset(x_plane[:, T // 2 : T].bitcast(I32), 0)
        nc.vector.memset(planes_raw[:].bitcast(I32), 0)
        nc.vector.memset(wb_plane[:].bitcast(I32), 0)

        nc.sync.dma_start(out=staged[:, 0 : R // 4], in_=w_scales[0].bitcast(I32))
        nc.scalar.dma_start(out=staged[:, R // 4 : R // 2], in_=w2_scales[0].bitcast(I32))
        nc.sync.dma_start(tokens[:], offs)
        nc.gpsimd.dma_start(out=offset[:], in_=bg.rearrange("(p t) o -> p (t o)", t=PACK))
        load_scale_row(nc.sync, x_plane, xt_scales, 0)
        load_scale_row(nc.sync, x_plane, xt_scales, 1)
        load_scale_row(nc.scalar, x_plane, xt_scales, 2)
        load_scale_row(nc.scalar, x_plane, xt_scales, 3)
        nc.sync.dma_start(out=x_words[:].bitcast(I32), in_=xt_words[0].rearrange("p t b -> p (t b)").bitcast(I32))
        nc.gpsimd.dma_start(out=slope[:], in_=sg.rearrange("(p t) o -> p (t o)", t=PACK))
        nc.sync.dma_start(out=w_raw[:].bitcast(I32), in_=w_words[0].bitcast(I32))
        nc.sync.dma_start(out=planes_raw[0:P:32, :].bitcast(I32), in_=staged[0:16:4, :])
        nc.sync.dma_start(out=planes_raw[1:P:32, :].bitcast(I32), in_=staged[1:16:4, :])
        nc.sync.dma_start(out=planes_raw[2:P:32, :].bitcast(I32), in_=staged[2:16:4, :])
        nc.sync.dma_start(out=planes_raw[3:P:32, :].bitcast(I32), in_=staged[3:16:4, :])
        nc.sync.dma_start(out=w2_raw[:].bitcast(I32), in_=w2_words[0].rearrange("p r b -> p (r b)").bitcast(I32))
        nc.sync.dma_start(gate_slots[:], offs2)
        nc.sync.dma_start(value_slots[:], offs3)
        nc.sync.dma_start(out=wb_codes[:].bitcast(I32), in_=wb_words[0].rearrange("p n b -> p (n b)").bitcast(I32))
        load_scale_row(nc.sync, wb_plane, wb_scales, 0)
        load_scale_row(nc.sync, wb_plane, wb_scales, 1)
        load_scale_row(nc.sync, wb_plane, wb_scales, 2)
        load_scale_row(nc.sync, wb_plane, wb_scales, 3)

        warm = keep.tile([P, 2], F32, name="warm")
        nc.vector.memset(warm[:, 0:1], 0.0)
        nc.scalar.activation(out=warm[:, 1:2], in_=warm[:, 0:1], func=ACT.Sigmoid)

        xg_plane = keep.tile([P, J], U8, name="xg_plane", align_bytes=64)
        xg_words = keep.tile([P, J], U32, name="xg_words", align_bytes=64)
        w_codes = keep.tile([P, R], U16, name="w_codes", align_bytes=64)
        w_plane = keep.tile([P, R], U8, name="w_plane", align_bytes=64)
        w2_codes = keep.tile([P, R], U32, name="w2_codes", tag="dealt", align_bytes=64)
        w2_plane = keep.tile([P, R], U8, name="w2_plane", align_bytes=64)

        def deal(copy, dst, src, first=0, last=PACK):
            copy(
                out=dst[:].rearrange("p (t m) -> p t m", t=PACK)[:, first:last, :],
                in_=src.rearrange("p (m t) -> p t m", t=PACK)[:, first:last, :],
            )

        nc.scalar.copy(
            out=w_codes[:].rearrange("p (t m) -> p m t", t=PACK), in_=w_raw[:].rearrange("p (m t) -> p m t", t=PACK)
        )
        nc.vector.tensor_copy(out=xg_plane[:], in_=x_plane[:].indirect(tokens[:]))
        nc.vector.tensor_copy(out=xg_words[:], in_=x_words[:].indirect(tokens[:]))
        deal(nc.vector.tensor_copy, w_plane, planes_raw[:, 0:R], 0, 2)
        deal(nc.vector.tensor_copy, w_plane, planes_raw[:, 0:R], 2, 4)
        deal(nc.vector.tensor_copy, w2_plane, planes_raw[:, R : 2 * R])
        nc.vector.tensor_copy(
            out=w2_codes[:].rearrange("p (t m) -> p m t", t=PACK), in_=w2_raw[:].rearrange("p (m t) -> p m t", t=PACK)
        )

        gate = keep.tile([P, PACK, O], F32, name="gate")
        value = keep.tile([P, PACK, O], F32, name="value")

        def product(codes, fmt, plane, t):
            cols = slice(t * P, (t + 1) * P)
            acc = psum.tile([P, J], F32, name="acc")
            nc.tensor.matmul_mx(
                out=acc[:],
                lhsT=codes[:, cols].bitcast(fmt),
                lhsT_scale=plane[:, cols],
                rhs=xg_words[:].bitcast(E4M3),
                rhs_scale=xg_plane[:],
                start=True,
                stop=True,
            )
            return acc

        a_accs = [product(w_codes, E2M1, w_plane, t) for t in range(PACK)]
        for t in range(PACK):
            a_rows = keep.tile([P, J], F32, name="a_rows%d" % t)
            copy = nc.scalar.copy if t < 2 else nc.vector.tensor_copy
            copy(out=a_rows[:], in_=a_accs[t][:])
            nc.scalar.activation(
                out=gate[:, t, :],
                in_=a_rows[:].indirect(gate_slots[:]),
                func=ACT.Sigmoid,
                bias=offset[:, t : t + 1],
                scale=slope[:, t : t + 1],
            )
        b_accs = [product(w2_codes, E5M2, w2_plane, t) for t in range(PACK)]
        for t in range(PACK):
            b_rows = keep.tile([P, J], F32, name="b_rows%d" % t)
            nc.vector.tensor_copy(out=b_rows[:], in_=b_accs[t][:])
            if t < PACK - 1:
                nc.scalar.activation(out=value[:, t, :], in_=b_rows[:].indirect(value_slots[:]), func=ACT.Copy)
            else:
                nc.vector.tensor_copy(out=value[:, t, :], in_=b_rows[:].indirect(value_slots[:]))

        hid = keep.tile([P, O, PACK], BF16, name="hid", align_bytes=64)
        hid_codes = keep.tile([P, O], U32, name="hid_codes", align_bytes=64)
        hid_plane = keep.tile([P, O], U8, name="hid_plane", align_bytes=64)
        halves = [slice(0, O // 2), slice(O // 2, O)]
        for half in halves:
            nc.vector.tensor_tensor(
                out=hid[:, half, :].rearrange("p (c i) t -> p c t i", i=4),
                in0=value[:, :, half].rearrange("p t (c i) -> p c t i", i=4),
                in1=gate[:, :, half].rearrange("p t (c i) -> p c t i", i=4),
                op=MULT,
            )
        for half in halves:
            nc.vector.quantize_mx(
                out=hid_codes[:, half].bitcast(E4M3),
                scales=hid_plane[:, half],
                in_=hid[:, half, :].rearrange("p o t -> p (o t)"),
            )

        for h in range(N // P):
            cols = slice(h * P, (h + 1) * P)
            acc = psum.tile([P, J], F32, name="acc")
            nc.tensor.matmul_mx(
                out=acc[:, 0:O],
                lhsT=wb_codes[:, cols].bitcast(E5M2),
                lhsT_scale=wb_plane[:, cols],
                rhs=hid_codes[:].bitcast(E4M3),
                rhs_scale=hid_plane[:],
                start=True,
                stop=True,
            )
            result = keep.tile([P, O], F32, name="result%d" % h)
            if h == 0:
                nc.scalar.copy(out=result[:], in_=acc[:, 0:O])
                nc.scalar.dma_start(out=out[cols, :], in_=result[:])
            else:
                nc.vector.tensor_copy(out=result[:], in_=acc[:, 0:O])
                nc.sync.dma_start(out=out[cols, :], in_=result[:])
